import numpy as np
import ml_dtypes


def mxq(x, axis, fmt="e4m3"):
    dtype, down = {"e4m3": (ml_dtypes.float8_e4m3fn, 7), "e5m2": (ml_dtypes.float8_e5m2, 14)}[fmt]
    v = np.moveaxis(np.asarray(x, np.float32).astype(ml_dtypes.bfloat16).astype(np.float64), axis, -1)
    blocks = v.reshape(v.shape[:-1] + (-1, 32))
    amax = np.abs(blocks).max(-1, keepdims=True)
    byte = np.maximum(np.where(amax > 0, np.frexp(amax)[1] - 1 + 127, 0) - down, 1)
    scale = np.exp2(byte - 127.0)
    codes = (blocks / scale).astype(np.float32).astype(dtype).astype(np.float64)
    return np.moveaxis((codes * scale).reshape(v.shape), -1, axis)


WIDE = False


def mx_kscale(k):
    if not WIDE:
        return np.ones(k)
    levels = np.array([10, -10, 5, -5, 0])
    if k % 512:
        return np.exp2(np.random.permutation(np.resize(levels, k // 32))).repeat(32)
    a = np.empty((k // 512, 16))
    for p in range(k // 512):
        a[p, :8] = np.random.permutation(np.resize(levels, 8))
        for g in range(8):
            far = levels[np.abs(levels - a[p, g]) >= 10]
            a[p, g + 8] = far[np.random.randint(len(far))]
    return np.exp2(a.ravel()).repeat(32)


def f64(x):
    return np.asarray(x).astype(np.float64)


def striped(idx):
    return np.tile(idx.reshape(-1, 16).T, (8, 1)).astype(np.uint16)


def unstriped(offs):
    return offs[:16].T.reshape(-1).astype(np.int64)


E2M1 = np.array([0.0, 0.5, 1.0, 1.5, 2.0, 3.0, 4.0, 6.0, -0.0, -0.5, -1.0, -1.5, -2.0, -3.0, -4.0, -6.0])


def pack_weight(w, fmt):
    k, n = w.shape
    w = f64(np.asarray(w, np.float32).astype(ml_dtypes.bfloat16)).reshape(k // 32, 32, n)
    amax = np.abs(w).max(1)
    if fmt == "e4m3":
        byte = np.frexp(amax)[1] - 1 + 127 - 7
    else:
        mant, ex = np.frexp(amax / 6.0)
        byte = np.where(mant > 0.5, ex, ex - 1) + 127
    byte = np.clip(np.where(amax > 0, byte, 1), 1, 254)
    scaled = (w * np.exp2(127.0 - byte)[:, None, :]).reshape(k, n).astype(np.float32)
    by_word = np.ascontiguousarray(scaled.reshape(k // 512, 128, 4, n).transpose(0, 1, 3, 2))
    if fmt == "e4m3":
        words = by_word.astype(ml_dtypes.float8_e4m3fn).view(np.uint8)
    else:
        c = by_word.astype(ml_dtypes.float4_e2m1fn).view(np.uint8) & 0xF
        words = (c[..., 0::2] | (c[..., 1::2] << 4)).reshape(k // 512, 128, 2 * n)
    return np.ascontiguousarray(words), np.ascontiguousarray(byte.astype(np.uint8).reshape(k // 512, 16, n))


def unpack_weight(words, scales, fmt):
    g, _, n = scales.shape
    words = np.ascontiguousarray(words).reshape(g, 128, n, -1)
    if fmt == "e4m3":
        vals = words.view(ml_dtypes.float8_e4m3fn).astype(np.float64)
    else:
        nib = np.empty((g, 128, n, 4), np.uint8)
        nib[..., 0::2] = words & 0xF
        nib[..., 1::2] = words >> 4
        vals = E2M1[nib]
    vals = vals * np.repeat(np.exp2(scales.astype(np.float64) - 127.0), 8, axis=1)[..., None]
    return vals.transpose(0, 1, 3, 2).reshape(g * 512, n)


def gelu(v):
    return 0.5 * v * (1.0 + np.tanh(np.sqrt(2.0 / np.pi) * (v + 0.044715 * v**3)))


def often(T, S):
    return np.random.permutation(T)[(T * np.random.uniform(0, 1, S) ** 4).astype(np.int64)]


def bf(x):
    return np.asarray(x, np.float32).astype(ml_dtypes.bfloat16)


def planes(Y):
    n, m = Y.shape
    b = f64(bf(Y)).reshape(n // 32, 32, m)
    amax = np.abs(b).max(1)
    byte = np.clip(np.where(amax > 0, np.frexp(amax)[1] - 1 + 127 - 7, 1), 1, 254)
    codes = (b * np.exp2(127.0 - byte)[:, None, :]).reshape(n, m).astype(np.float32).astype(ml_dtypes.float8_e4m3fn).view(np.uint8)
    words = codes.reshape(n // 512, 128, 4, m).transpose(0, 1, 3, 2)
    return np.ascontiguousarray(words), np.ascontiguousarray(byte.astype(np.uint8).reshape(n // 512, 16, m))


T, S, P, K, K2, H, N = 4096, 1024, 512, 1024, 512, 1024, 512

def setup_inputs():
    n = np.random.standard_normal
    s, s2, s3 = mx_kscale(K)[:, None], mx_kscale(K2)[:, None], mx_kscale(K2)[:, None]
    u = mx_kscale(H)[:, None]
    d = {}
    d["tab_words"], d["tab_scales"] = pack_weight(n((K, T)) * s, "e4m3")
    d["tab2_words"], d["tab2_scales"] = pack_weight(n((K2, T)) * s2, "e4m3")
    d["tab3_words"], d["tab3_scales"] = pack_weight(n((K2, T)) * s3, "e4m3")
    d["offs"] = striped(np.random.permutation(T)[:S])
    d["offs2"] = striped(np.random.permutation(T)[:S])
    d["offs3"] = striped(np.random.permutation(T)[:S])
    d["pos1"] = striped(np.random.permutation(S)[:P])
    d["pos2"] = striped(often(S, P))
    d["pos3"] = striped(often(S, P))
    d["w1"] = (1.6 * n((K, H)) / K**0.5 / s).astype(np.float32)
    d["w2_words"], d["w2_scales"] = pack_weight(0.8 * n((K2, H)) / K2**0.5 / s2 * u.T, "e2m1")
    d["w3"] = (0.8 * n((K2, H)) / K2**0.5 / s3 * u.T).astype(np.float32)
    d["gn"] = (2.5 * np.exp(0.3 * n(H)) * u[:, 0]).astype(np.float32)
    d["w4_words"], d["w4_scales"] = pack_weight(n((H, N)) / H**0.5 / u * np.exp(0.8 * n(N)), "e4m3")
    return d

def reference(tab_words, tab_scales, tab2_words, tab2_scales, tab3_words, tab3_scales, offs, offs2, offs3,
              pos1, pos2, pos3, w1, w2_words, w2_scales, w3, gn, w4_words, w4_scales):
    v = unpack_weight(tab_words, tab_scales, "e4m3")[:, unstriped(offs)]
    v2 = unpack_weight(tab2_words, tab2_scales, "e4m3")[:, unstriped(offs2)]
    v3 = unpack_weight(tab3_words, tab3_scales, "e4m3")[:, unstriped(offs3)]
    a = mxq(f64(w1), 0, "e4m3").T @ v
    b = unpack_weight(w2_words, w2_scales, "e2m1").T @ v2
    d = mxq(f64(w3), 0, "e4m3").T @ v3
    sat = f64(gn)[:, None] / (1.0 + np.abs(a[:, unstriped(pos1)]))
    z = sat + b[:, unstriped(pos2)] - d[:, unstriped(pos3)]
    y = unpack_weight(w4_words, w4_scales, "e4m3").T @ mxq(z, 0, "e4m3")
    words, scales = planes(y)
    return y, words, scales

@@ -1,0 +1,250 @@
+from contextlib import ExitStack
+
+import concourse.mybir as mybir
+
+F32 = mybir.dt.float32
+BF16 = mybir.dt.bfloat16
+I32 = mybir.dt.int32
+U32 = mybir.dt.uint32
+U16 = mybir.dt.uint16
+U8 = mybir.dt.uint8
+FP8X4 = mybir.dt.float8_e4m3fn_x4
+FP4X4 = mybir.dt.float4_e2m1fn_x4
+ACT = mybir.ActivationFunctionType
+ALU = mybir.AluOpType
+
+FLOPS = 4831838208
+
+P = 128
+PACK = 4
+T = 4096
+S = 1024
+J = 512
+BANK = 512
+GROUP = 512
+HALF = J // 2
+
+
+def tile_list_catalyst_cycle_oven_kernel(
+    tc, tab_words, tab_scales, tab2_words, tab2_scales, tab3_words, tab3_scales, offs, offs2, offs3,
+    pos1, pos2, pos3, w1, w2_words, w2_scales, w3, gn, w4_words, w4_scales, out_0, out_1, out_2,
+):
+    nc = tc.nc
+    with ExitStack() as ctx:
+        held = ctx.enter_context(tc.tile_pool(name="held", bufs=1))
+        ring = ctx.enter_context(tc.tile_pool(name="ring", bufs=2))
+        psum = ctx.enter_context(tc.psum_pool(name="psum", bufs=8))
+
+        def load_list(src, name):
+            lst = held.tile(list(src.shape), U16, name=name)
+            nc.sync.dma_start(lst[:], src)
+            return lst
+
+        def zeroed_plane(width, name):
+            plane = held.tile([P, width], U8, name=name, align_bytes=64)
+            nc.vector.memset(plane[:].bitcast(I32), 0)
+            return plane
+
+        def load_scale_rows(queue, plane, src, first_row):
+            passes = src.shape[0]
+            for q in range(4):
+                row = 32 * q + first_row
+                queue.dma_start(plane[row : row + 4 * passes, :].bitcast(I32), src[:, 4 * q : 4 * q + 4, :].bitcast(I32))
+
+        def load_table(src, a, name):
+            words = ring.tile([P, T], U32, name=name, tag="table", bufs=3)
+            nc.sync.dma_start(words[:].bitcast(I32), src[a].rearrange("p n t -> p (n t)").bitcast(I32))
+            return words
+
+        def load_weight(src, a, g, name):
+            raw = ring.tile([P, PACK, GROUP], F32, name=name, tag="raw", bufs=3)
+            rows = src[GROUP * a : GROUP * (a + 1), GROUP * g : GROUP * (g + 1)]
+            nc.sync.dma_start(raw[:], rows.rearrange("(p j) c -> p j c", j=PACK))
+            return raw
+
+        def gather_scales(plane, lst, name):
+            picked = held.tile([P, S], U8, name=name, align_bytes=64)
+            nc.vector.tensor_copy(picked[:], plane[:].indirect(lst[:]))
+            return picked
+
+        def gather_words(words, lst, name):
+            halves = []
+            for h in range(2):
+                picked = held.tile([P, BANK], U32, name=name + str(h), align_bytes=64)
+                nc.vector.tensor_copy(picked[:], words[:].indirect(lst[:, 32 * h : 32 * (h + 1)]))
+                halves.append(picked)
+            return halves
+
+        def quantize_weight(raw, name):
+            grouped = ring.tile([P, PACK * GROUP], BF16, name="grouped", tag="grouped", bufs=3, align_bytes=64)
+            dst = grouped[:].rearrange("p (t m j) -> p m j t", t=PACK, j=PACK)
+            src = raw[:].rearrange("p j (m t) -> p m j t", t=PACK)
+            dst = grouped[:].rearrange("p (t m j) -> p t m j", t=PACK, j=PACK)
+            src = raw[:].rearrange("p j (m t) -> p t m j", t=PACK)
+            nc.gpsimd.tensor_scalar(dst, src, 1.0, 0.0, ALU.mult, ALU.add)
+            codes = held.tile([P, GROUP], U32, name=name + "_codes", align_bytes=64)
+            scales = held.tile([P, GROUP], U8, name=name + "_scales", align_bytes=64)
+            nc.vector.quantize_mx(out=codes[:].bitcast(FP8X4), scales=scales[:], in_=grouped[:])
+            return codes, scales
+
+        def first_stage(passes, func):
+            window = ring.tile([P, S], F32, name="window", tag="window", bufs=6)
+            for h in range(2):
+                acc = psum.tile([P, BANK], F32, name="acc", tag="acc")
+                for a, (w_codes, w_scales, v_halves, v_scales) in enumerate(passes):
+                    nc.tensor.matmul_mx(
+                        out=acc[:], lhsT=w_codes, lhsT_scale=w_scales, rhs=v_halves[h][:].bitcast(FP8X4),
+                        rhs_scale=v_scales[:, BANK * h : BANK * (h + 1)], start=(a == 0), stop=(a == len(passes) - 1),
+                    )
+                nc.scalar.activation(window[:, BANK * h : BANK * (h + 1)], acc[:], func)
+            return window
+
+        tab2_plane = zeroed_plane(T, "tab2_plane")
+        w2_plane = zeroed_plane(S, "w2_plane")
+        tab_plane = zeroed_plane(T, "tab_plane")
+        tab3_plane = zeroed_plane(T, "tab3_plane")
+        w4_plane = zeroed_plane(GROUP, "w4_plane")
+
+        offs2_sb = load_list(offs2, "offs2_sb")
+        pos2_sb = load_list(pos2, "pos2_sb")
+        offs_sb = load_list(offs, "offs_sb")
+        pos1_sb = load_list(pos1, "pos1_sb")
+        offs3_sb = load_list(offs3, "offs3_sb")
+        pos3_sb = load_list(pos3, "pos3_sb")
+        w2_raw = held.tile([P, 2 * S], U8, name="w2_raw")
+        nc.sync.dma_start(w2_raw[:].bitcast(I32), w2_words[0].bitcast(I32))
+        tab2_sb = ring.tile([P, T], U32, name="tab2_sb", tag="table", bufs=3)
+        tab2_src = tab2_words[0].rearrange("p n t -> p (n t)").bitcast(I32)
+        nc.sync.dma_start(tab2_sb[:, : T // 2].bitcast(I32), tab2_src[:, : T // 2])
+        load_scale_rows(nc.sync, tab2_plane, tab2_scales, 0)
+        nc.sync.dma_start(tab2_sb[:, T // 2 :].bitcast(I32), tab2_src[:, T // 2 :])
+        load_scale_rows(nc.sync, w2_plane, w2_scales, 0)
+        tab_sb = [ring.tile([P, T], U32, name="tab_sb", tag="table", bufs=3)]
+        tab_src = tab_words[0].rearrange("p n t -> p (n t)").bitcast(I32)
+        nc.sync.dma_start(tab_sb[0][:, : T // 2].bitcast(I32), tab_src[:, : T // 2])
+        load_scale_rows(nc.sync, tab_plane, tab_scales, 4)
+        nc.sync.dma_start(tab_sb[0][:, T // 2 :].bitcast(I32), tab_src[:, T // 2 :])
+        tab_sb.append(load_table(tab_words, 1, "tab_sb"))
+        w1_raw = {(a, 0): load_weight(w1, a, 0, "w1_raw") for a in range(2)}
+        gain = held.tile([P, 2, PACK], F32, name="gain")
+        nc.sync.dma_start(gain[:], gn.rearrange("(g p t) -> p g t", g=2, t=PACK))
+        for a in range(2):
+            w1_raw[a, 1] = load_weight(w1, a, 1, "w1_raw")
+        load_scale_rows(nc.sync, tab3_plane, tab3_scales, 12)
+        tab3_sb = load_table(tab3_words, 0, "tab3_sb")
+        w3_raw = [load_weight(w3, 0, g, "w3_raw") for g in range(2)]
+        load_scale_rows(nc.sync, w4_plane, w4_scales, 0)
+        w4_raw = held.tile([P, 2, GROUP], I32, name="w4_raw")
+        nc.sync.dma_start(w4_raw[:], w4_words.rearrange("a p n t -> p a (n t)").bitcast(I32))
+        warm = held.tile([P, 1], F32, name="warm")
+        nc.vector.memset(warm[:], 1.0)
+        nc.scalar.activation(warm[:], warm[:], ACT.Abs_reciprocal_sqrt, bias=1.0)
+
+        v2_scales = gather_scales(tab2_plane, offs2_sb, "v2_scales")
+        w2_codes = held.tile([P, 2 * S], U8, name="w2_codes", align_bytes=64)
+        nc.vector.tensor_copy(
+            w2_codes[:].rearrange("p (g t m b) -> p g m t b", g=2, t=PACK, b=2),
+            w2_raw[:].rearrange("p (g m t b) -> p g m t b", g=2, t=PACK, b=2),
+        )
+        w2_dealt = held.tile([P, S], U8, name="w2_dealt", align_bytes=64)
+        nc.gpsimd.tensor_copy(
+            w2_dealt[:].rearrange("p (g t m) -> p g t m", g=2, t=PACK),
+            w2_plane[:].rearrange("p (g m t) -> p g t m", g=2, t=PACK),
+        )
+        v2 = gather_words(tab2_sb, offs2_sb, "v2")
+        partial = [held.tile([P, PACK, J], F32, name="partial" + str(g)) for g in range(2)]
+        for g in range(2):
+            for t in range(PACK):
+                col = GROUP * g + P * t
+                w_codes = w2_codes[:, 2 * col : 2 * (col + P)].bitcast(FP4X4)
+                window = first_stage([(w_codes, w2_dealt[:, col : col + P], v2, v2_scales)], ACT.Copy)
+                nc.vector.tensor_copy(partial[g][:, t, :], window[:].indirect(pos2_sb[:]))
+
+        v_scales = gather_scales(tab_plane, offs_sb, "v_scales")
+        v = [gather_words(tab_sb[a], offs_sb, "v" + str(a)) for a in range(2)]
+        picked_a = {}
+        w1_all = [[quantize_weight(w1_raw[a, g], "w1_" + str(a) + str(g)) for a in range(2)] for g in range(2)]
+        for g in range(2):
+            w1_q = w1_all[g]
+            for t in range(PACK):
+                cols = slice(P * t, P * (t + 1))
+                passes = [
+                    (w1_q[a][0][:, cols].bitcast(FP8X4), w1_q[a][1][:, cols], v[a], v_scales[4 + 4 * a :, :])
+                    for a in range(2)
+                ]
+                window = first_stage(passes, ACT.Abs)
+                sat = ring.tile([P, J], F32, name="sat", tag="sat", bufs=8)
+                nc.vector.tensor_copy(sat[:], window[:].indirect(pos1_sb[:]))
+                picked_a[g, t] = sat
+
+        v3_scales = gather_scales(tab3_plane, offs3_sb, "v3_scales")
+        v3 = gather_words(tab3_sb, offs3_sb, "v3")
+        w4_codes = held.tile([P, 2, GROUP], I32, name="w4_codes", align_bytes=64)
+        nc.gpsimd.tensor_copy(
+            w4_codes[:].rearrange("p a (t m) -> p a t m", t=PACK), w4_raw[:].rearrange("p a (m t) -> p a t m", t=PACK)
+        )
+        w4_dealt = held.tile([P, GROUP], U8, name="w4_dealt", align_bytes=64)
+        nc.gpsimd.tensor_copy(
+            w4_dealt[:].rearrange("p (t m) -> p t m", t=PACK), w4_plane[:].rearrange("p (m t) -> p t m", t=PACK)
+        )
+        w3_q = [quantize_weight(w3_raw[g], "w3_" + str(g)) for g in range(2)]
+        z_q = {}
+        for g in range(2):
+            windows = []
+            for t in range(PACK):
+                cols = slice(P * t, P * (t + 1))
+                sat = picked_a[g, t]
+                nc.scalar.activation(sat[:], sat[:], ACT.Abs_reciprocal_sqrt, bias=1.0)
+                nc.scalar.activation(sat[:], sat[:], ACT.Square)
+                nc.vector.scalar_tensor_tensor(
+                    partial[g][:, t, :], sat[:], gain[:, g, t : t + 1], partial[g][:, t, :], ALU.mult, ALU.add
+                )
+                passes = [(w3_q[g][0][:, cols].bitcast(FP8X4), w3_q[g][1][:, cols], v3, v3_scales[12:, :])]
+                windows.append(first_stage(passes, ACT.Copy))
+            pick_width, join_width = ((512, 256), (128, 128))[g]
+            for c0 in range(0, J, pick_width):
+                picked_d = ring.tile([P, PACK, pick_width], F32, name="picked_d", tag="picked_d" + str(g), bufs=(1, 2)[g])
+                for t in range(PACK):
+                    nc.vector.tensor_copy(
+                        picked_d[:, t, :], windows[t][:].indirect(pos3_sb[:, c0 // 16 : (c0 + pick_width) // 16])
+                    )
+                for c1 in range(0, pick_width, join_width):
+                    z = ring.tile([P, PACK * join_width], BF16, name="z", tag="z", bufs=2, align_bytes=64)
+                    nc.vector.tensor_tensor(
+                        z[:].rearrange("p (c i t) -> p c t i", i=4, t=PACK),
+                        partial[g][:, :, c0 + c1 : c0 + c1 + join_width].rearrange("p t (c i) -> p c t i", i=4),
+                        picked_d[:, :, c1 : c1 + join_width].rearrange("p t (c i) -> p c t i", i=4),
+                        ALU.subtract,
+                    )
+                    z_codes = held.tile([P, join_width], U32, name="z_codes" + str(g) + str(c0 + c1), align_bytes=64)
+                    z_scales = held.tile([P, join_width], U8, name="z_scales" + str(g) + str(c0 + c1), align_bytes=64)
+                    nc.vector.quantize_mx(out=z_codes[:].bitcast(FP8X4), scales=z_scales[:], in_=z[:])
+                    for c2 in range(0, join_width, P):
+                        z_q[g, (c0 + c1 + c2) // P] = (z_codes[:, c2 : c2 + P], z_scales[:, c2 : c2 + P])
+
+        out_rows = out_0.rearrange("(p t) m -> p t m", t=PACK)
+        out_words = out_1[0].rearrange("p m t -> p (m t)").bitcast(I32)
+        y_scales = held.tile([P, J], U8, name="y_scales", align_bytes=64)
+        for c in range(J // P):
+            cols = slice(P * c, P * (c + 1))
+            acc = psum.tile([P, PACK, P], F32, name="y_acc", tag="acc")
+            for t in range(PACK):
+                for g in (1, 0):
+                    nc.tensor.matmul_mx(
+                        out=acc[:, t, :], lhsT=w4_codes[:, g, P * t : P * (t + 1)].bitcast(FP8X4),
+                        lhsT_scale=w4_dealt[4 * g :, P * t : P * (t + 1)], rhs=z_q[g, c][0].bitcast(FP8X4),
+                        rhs_scale=z_q[g, c][1], start=(g == 1), stop=(g == 0),
+                    )
+            y_bf = ring.tile([P, P, PACK], BF16, name="y_bf", tag="y_bf", bufs=4, align_bytes=64)
+            nc.scalar.copy(y_bf[:], acc[:].rearrange("p t m -> p m t"))
+            y = ring.tile([P, PACK, P], F32, name="y", tag="y", bufs=4)
+            nc.scalar.copy(y[:], acc[:])
+            nc.sync.dma_start(out_rows[:, :, cols], y[:])
+            y_codes = held.tile([P, P], U32, name="y_codes" + str(c), align_bytes=64)
+            nc.vector.quantize_mx(
+                out=y_codes[:].bitcast(FP8X4), scales=y_scales[:, cols], in_=y_bf[:].rearrange("p m t -> p (m t)")
+            )
+            nc.sync.dma_start(out_words[:, cols], y_codes[:].bitcast(I32))
+        for q in range(4):
+            queue = nc.sync if q % 2 == 0 else nc.scalar
+            queue.dma_start(out_2[0, 4 * q : 4 * q + 4, :].bitcast(I32), y_scales[32 * q : 32 * q + 4, :].bitcast(I32))

@@ -52,12 +52,12 @@ def tile_list_catalyst_cycle_oven_kernel(
                 queue.dma_start(plane[row : row + 4 * passes, :].bitcast(I32), src[:, 4 * q : 4 * q + 4, :].bitcast(I32))
 
         def load_table(src, a, name):
-            words = ring.tile([P, T], U32, name=name, tag="table", bufs=3)
+            words = ring.tile([P, T], U32, name=name, tag="table", bufs=2)
             nc.sync.dma_start(words[:].bitcast(I32), src[a].rearrange("p n t -> p (n t)").bitcast(I32))
             return words
 
         def load_weight(src, a, g, name):
-            raw = ring.tile([P, PACK, GROUP], F32, name=name, tag="raw", bufs=3)
+            raw = ring.tile([P, PACK, GROUP], F32, name=name, tag="raw", bufs=4)
             rows = src[GROUP * a : GROUP * (a + 1), GROUP * g : GROUP * (g + 1)]
             nc.sync.dma_start(raw[:], rows.rearrange("(p j) c -> p j c", j=PACK))
             return raw
@@ -75,13 +75,12 @@ def tile_list_catalyst_cycle_oven_kernel(
                 halves.append(picked)
             return halves
 
-        def quantize_weight(raw, name):
-            grouped = ring.tile([P, PACK * GROUP], BF16, name="grouped", tag="grouped", bufs=3, align_bytes=64)
-            dst = grouped[:].rearrange("p (t m j) -> p m j t", t=PACK, j=PACK)
-            src = raw[:].rearrange("p j (m t) -> p m j t", t=PACK)
-            dst = grouped[:].rearrange("p (t m j) -> p t m j", t=PACK, j=PACK)
-            src = raw[:].rearrange("p j (m t) -> p t m j", t=PACK)
-            nc.gpsimd.tensor_scalar(dst, src, 1.0, 0.0, ALU.mult, ALU.add)
+        def quantize_weight(raw, name, copy):
+            grouped = ring.tile([P, PACK * GROUP], BF16, name="grouped", tag="grouped", bufs=4, align_bytes=64)
+            copy(
+                grouped[:].rearrange("p (u e m j) -> p u m j e", u=2, e=2, j=PACK),
+                raw[:].rearrange("p j (m u e) -> p u m j e", u=2, e=2),
+            )
             codes = held.tile([P, GROUP], U32, name=name + "_codes", align_bytes=64)
             scales = held.tile([P, GROUP], U8, name=name + "_scales", align_bytes=64)
             nc.vector.quantize_mx(out=codes[:].bitcast(FP8X4), scales=scales[:], in_=grouped[:])
@@ -113,13 +112,13 @@ def tile_list_catalyst_cycle_oven_kernel(
         pos3_sb = load_list(pos3, "pos3_sb")
         w2_raw = held.tile([P, 2 * S], U8, name="w2_raw")
         nc.sync.dma_start(w2_raw[:].bitcast(I32), w2_words[0].bitcast(I32))
-        tab2_sb = ring.tile([P, T], U32, name="tab2_sb", tag="table", bufs=3)
+        tab2_sb = ring.tile([P, T], U32, name="tab2_sb", tag="table", bufs=2)
         tab2_src = tab2_words[0].rearrange("p n t -> p (n t)").bitcast(I32)
         nc.sync.dma_start(tab2_sb[:, : T // 2].bitcast(I32), tab2_src[:, : T // 2])
         load_scale_rows(nc.sync, tab2_plane, tab2_scales, 0)
         nc.sync.dma_start(tab2_sb[:, T // 2 :].bitcast(I32), tab2_src[:, T // 2 :])
         load_scale_rows(nc.sync, w2_plane, w2_scales, 0)
-        tab_sb = [ring.tile([P, T], U32, name="tab_sb", tag="table", bufs=3)]
+        tab_sb = [ring.tile([P, T], U32, name="tab_sb", tag="table", bufs=2)]
         tab_src = tab_words[0].rearrange("p n t -> p (n t)").bitcast(I32)
         nc.sync.dma_start(tab_sb[0][:, : T // 2].bitcast(I32), tab_src[:, : T // 2])
         load_scale_rows(nc.sync, tab_plane, tab_scales, 4)
@@ -130,8 +129,8 @@ def tile_list_catalyst_cycle_oven_kernel(
         nc.sync.dma_start(gain[:], gn.rearrange("(g p t) -> p g t", g=2, t=PACK))
         for a in range(2):
             w1_raw[a, 1] = load_weight(w1, a, 1, "w1_raw")
-        load_scale_rows(nc.sync, tab3_plane, tab3_scales, 12)
         tab3_sb = load_table(tab3_words, 0, "tab3_sb")
+        load_scale_rows(nc.sync, tab3_plane, tab3_scales, 12)
         w3_raw = [load_weight(w3, 0, g, "w3_raw") for g in range(2)]
         load_scale_rows(nc.sync, w4_plane, w4_scales, 0)
         w4_raw = held.tile([P, 2, GROUP], I32, name="w4_raw")
@@ -143,11 +142,11 @@ def tile_list_catalyst_cycle_oven_kernel(
         v2_scales = gather_scales(tab2_plane, offs2_sb, "v2_scales")
         w2_codes = held.tile([P, 2 * S], U8, name="w2_codes", align_bytes=64)
         nc.vector.tensor_copy(
-            w2_codes[:].rearrange("p (g t m b) -> p g m t b", g=2, t=PACK, b=2),
-            w2_raw[:].rearrange("p (g m t b) -> p g m t b", g=2, t=PACK, b=2),
+            w2_codes[:].rearrange("p (g t m b) -> p g t m b", g=2, t=PACK, b=2),
+            w2_raw[:].rearrange("p (g m t b) -> p g t m b", g=2, t=PACK, b=2),
         )
         w2_dealt = held.tile([P, S], U8, name="w2_dealt", align_bytes=64)
-        nc.gpsimd.tensor_copy(
+        nc.vector.tensor_copy(
             w2_dealt[:].rearrange("p (g t m) -> p g t m", g=2, t=PACK),
             w2_plane[:].rearrange("p (g m t) -> p g t m", g=2, t=PACK),
         )
@@ -163,14 +162,14 @@ def tile_list_catalyst_cycle_oven_kernel(
         v_scales = gather_scales(tab_plane, offs_sb, "v_scales")
         v = [gather_words(tab_sb[a], offs_sb, "v" + str(a)) for a in range(2)]
         picked_a = {}
-        w1_all = [[quantize_weight(w1_raw[a, g], "w1_" + str(a) + str(g)) for a in range(2)] for g in range(2)]
+        w1_all = [[quantize_weight(w1_raw[a, g], "w1_" + str(a) + str(g), nc.scalar.copy) for a in range(2)] for g in range(2)]
         for g in range(2):
             w1_q = w1_all[g]
             for t in range(PACK):
                 cols = slice(P * t, P * (t + 1))
                 passes = [
                     (w1_q[a][0][:, cols].bitcast(FP8X4), w1_q[a][1][:, cols], v[a], v_scales[4 + 4 * a :, :])
-                    for a in range(2)
+                    for a in (1, 0)
                 ]
                 window = first_stage(passes, ACT.Abs)
                 sat = ring.tile([P, J], F32, name="sat", tag="sat", bufs=8)
@@ -180,14 +179,15 @@ def tile_list_catalyst_cycle_oven_kernel(
         v3_scales = gather_scales(tab3_plane, offs3_sb, "v3_scales")
         v3 = gather_words(tab3_sb, offs3_sb, "v3")
         w4_codes = held.tile([P, 2, GROUP], I32, name="w4_codes", align_bytes=64)
-        nc.gpsimd.tensor_copy(
-            w4_codes[:].rearrange("p a (t m) -> p a t m", t=PACK), w4_raw[:].rearrange("p a (m t) -> p a t m", t=PACK)
+        nc.vector.tensor_copy(
+            w4_codes[:].rearrange("p a (u e m) -> p a u m e", u=2, e=2),
+            w4_raw[:].rearrange("p a (m u e) -> p a u m e", u=2, e=2),
         )
         w4_dealt = held.tile([P, GROUP], U8, name="w4_dealt", align_bytes=64)
-        nc.gpsimd.tensor_copy(
+        nc.vector.tensor_copy(
             w4_dealt[:].rearrange("p (t m) -> p t m", t=PACK), w4_plane[:].rearrange("p (m t) -> p t m", t=PACK)
         )
-        w3_q = [quantize_weight(w3_raw[g], "w3_" + str(g)) for g in range(2)]
+        w3_q = [quantize_weight(w3_raw[g], "w3_" + str(g), (nc.vector.tensor_copy, nc.scalar.copy)[g]) for g in range(2)]
         z_q = {}
         for g in range(2):
             windows = []
@@ -205,17 +205,18 @@ def tile_list_catalyst_cycle_oven_kernel(
             for c0 in range(0, J, pick_width):
                 picked_d = ring.tile([P, PACK, pick_width], F32, name="picked_d", tag="picked_d" + str(g), bufs=(1, 2)[g])
                 for t in range(PACK):
-                    nc.vector.tensor_copy(
-                        picked_d[:, t, :], windows[t][:].indirect(pos3_sb[:, c0 // 16 : (c0 + pick_width) // 16])
+                    nc.vector.tensor_tensor(
+                        picked_d[:, t, :], windows[t][:].indirect(pos3_sb[:, c0 // 16 : (c0 + pick_width) // 16]),
+                        partial[g][:, t, c0 : c0 + pick_width], ALU.subtract,
                     )
                 for c1 in range(0, pick_width, join_width):
                     z = ring.tile([P, PACK * join_width], BF16, name="z", tag="z", bufs=2, align_bytes=64)
-                    nc.vector.tensor_tensor(
-                        z[:].rearrange("p (c i t) -> p c t i", i=4, t=PACK),
-                        partial[g][:, :, c0 + c1 : c0 + c1 + join_width].rearrange("p t (c i) -> p c t i", i=4),
-                        picked_d[:, :, c1 : c1 + join_width].rearrange("p t (c i) -> p c t i", i=4),
-                        ALU.subtract,
-                    )
+                    z_out = z[:].rearrange("p (c i t) -> p c t i", i=2, t=PACK)
+                    z_in = picked_d[:, :, c1 : c1 + join_width].rearrange("p t (c i) -> p c t i", i=2)
+                    if g in ():
+                        nc.scalar.activation(z_out, z_in, ACT.Copy, scale=-1.0)
+                    else:
+                        nc.vector.tensor_scalar(z_out, z_in, -1.0, None, ALU.mult)
                     z_codes = held.tile([P, join_width], U32, name="z_codes" + str(g) + str(c0 + c1), align_bytes=64)
                     z_scales = held.tile([P, join_width], U8, name="z_scales" + str(g) + str(c0 + c1), align_bytes=64)
                     nc.vector.quantize_mx(out=z_codes[:].bitcast(FP8X4), scales=z_scales[:], in_=z[:])
@@ -236,9 +237,15 @@ def tile_list_catalyst_cycle_oven_kernel(
                         rhs_scale=z_q[g, c][1], start=(g == 1), stop=(g == 0),
                     )
             y_bf = ring.tile([P, P, PACK], BF16, name="y_bf", tag="y_bf", bufs=4, align_bytes=64)
-            nc.scalar.copy(y_bf[:], acc[:].rearrange("p t m -> p m t"))
             y = ring.tile([P, PACK, P], F32, name="y", tag="y", bufs=4)
-            nc.scalar.copy(y[:], acc[:])
+            if c >= 0:
+                nc.scalar.copy(y[:], acc[:])
+                nc.vector.tensor_copy(
+                    y_bf[:].rearrange("p (c i) t -> p c t i", i=2), y[:].rearrange("p t (c i) -> p c t i", i=2)
+                )
+            else:
+                nc.scalar.copy(y_bf[:], acc[:].rearrange("p t m -> p m t"))
+                nc.scalar.copy(y[:], acc[:])
             nc.sync.dma_start(out_rows[:, :, cols], y[:])
             y_codes = held.tile([P, P], U32, name="y_codes" + str(c), align_bytes=64)
             nc.vector.quantize_mx(

@@ -17,12 +17,26 @@ FLOPS = 4831838208
 
 P = 128
 PACK = 4
+GROUP = P * PACK
 T = 4096
 S = 1024
 J = 512
 BANK = 512
-GROUP = 512
-HALF = J // 2
+ENTRIES = 16
+SLICES = 2 * PACK
+
+V_ROW, V3_ROW = 4, 12
+
+TABLE_SLOTS = 3
+RAW_SLOTS = 4
+ROUNDED_SLOTS = 4
+WINDOW_SLOTS = 7
+
+TAB2_FIRST = T // 4
+W1_FIRST_AFTER = 5
+W3_EVERY = 3
+SAT_AHEAD = 2
+Y_BY_SCALAR = 2
 
 
 def tile_list_catalyst_cycle_oven_kernel(
@@ -40,69 +54,77 @@ def tile_list_catalyst_cycle_oven_kernel(
             nc.sync.dma_start(lst[:], src)
             return lst
 
-        def zeroed_plane(width, name):
-            plane = held.tile([P, width], U8, name=name, align_bytes=64)
-            nc.vector.memset(plane[:].bitcast(I32), 0)
-            return plane
+        def zeroed_scale_tile(width, name):
+            tile = held.tile([P, width], U8, name=name, align_bytes=64)
+            nc.vector.memset(tile[:].bitcast(I32), 0)
+            return tile
 
-        def load_scale_rows(queue, plane, src, first_row):
+        def load_scale_rows(tile, src, first_row):
             passes = src.shape[0]
-            for q in range(4):
-                row = 32 * q + first_row
-                queue.dma_start(plane[row : row + 4 * passes, :].bitcast(I32), src[:, 4 * q : 4 * q + 4, :].bitcast(I32))
+            for quad in range(4):
+                row = 32 * quad + first_row
+                nc.sync.dma_start(
+                    tile[row : row + 4 * passes, :].bitcast(I32), src[:, 4 * quad : 4 * quad + 4, :].bitcast(I32)
+                )
 
-        def load_table(src, a, name):
-            words = ring.tile([P, T], U32, name=name, tag="table", bufs=2)
-            nc.sync.dma_start(words[:].bitcast(I32), src[a].rearrange("p n t -> p (n t)").bitcast(I32))
-            return words
+        def table_tile(name):
+            return ring.tile([P, T], U32, name=name, tag="table", bufs=TABLE_SLOTS, align_bytes=64)
 
-        def load_weight(src, a, g, name):
-            raw = ring.tile([P, PACK, GROUP], F32, name=name, tag="raw", bufs=4)
-            rows = src[GROUP * a : GROUP * (a + 1), GROUP * g : GROUP * (g + 1)]
-            nc.sync.dma_start(raw[:], rows.rearrange("(p j) c -> p j c", j=PACK))
+        def load_table_columns(words, src, kp, first, last):
+            columns = src[kp].rearrange("p col i -> p (col i)").bitcast(I32)
+            nc.sync.dma_start(words[:, first:last].bitcast(I32), columns[:, first:last])
+
+        def load_weight(src, kp, g, name):
+            raw = ring.tile([P, PACK, GROUP], F32, name=name, tag="raw", bufs=RAW_SLOTS)
+            rows = src[GROUP * kp : GROUP * (kp + 1), GROUP * g : GROUP * (g + 1)]
+            nc.sync.dma_start(raw[:], rows.rearrange("(p i) col -> p i col", i=PACK))
             return raw
 
-        def gather_scales(plane, lst, name):
+        def gather_scales(tile, lst, name):
             picked = held.tile([P, S], U8, name=name, align_bytes=64)
-            nc.vector.tensor_copy(picked[:], plane[:].indirect(lst[:]))
+            nc.vector.tensor_copy(picked[:], tile[:].indirect(lst[:]))
             return picked
 
         def gather_words(words, lst, name):
             halves = []
+            width = BANK // ENTRIES
             for h in range(2):
                 picked = held.tile([P, BANK], U32, name=name + str(h), align_bytes=64)
-                nc.vector.tensor_copy(picked[:], words[:].indirect(lst[:, 32 * h : 32 * (h + 1)]))
+                nc.vector.tensor_copy(picked[:], words[:].indirect(lst[:, width * h : width * (h + 1)]))
                 halves.append(picked)
             return halves
 
-        def quantize_weight(raw, name, copy):
-            grouped = ring.tile([P, PACK * GROUP], BF16, name="grouped", tag="grouped", bufs=4, align_bytes=64)
-            copy(
-                grouped[:].rearrange("p (u e m j) -> p u m j e", u=2, e=2, j=PACK),
-                raw[:].rearrange("p j (m u e) -> p u m j e", u=2, e=2),
+        def quantize_weight(raw, name):
+            rounded = ring.tile([P, PACK * GROUP], BF16, name="rounded", tag="rounded", bufs=ROUNDED_SLOTS, align_bytes=64)
+            nc.scalar.copy(
+                rounded[:].rearrange("p (u e w i) -> p u w i e", u=2, e=2, i=PACK),
+                raw[:].rearrange("p i (w u e) -> p u w i e", u=2, e=2),
             )
             codes = held.tile([P, GROUP], U32, name=name + "_codes", align_bytes=64)
             scales = held.tile([P, GROUP], U8, name=name + "_scales", align_bytes=64)
-            nc.vector.quantize_mx(out=codes[:].bitcast(FP8X4), scales=scales[:], in_=grouped[:])
+            nc.vector.quantize_mx(out=codes[:].bitcast(FP8X4), scales=scales[:], in_=rounded[:])
             return codes, scales
 
         def first_stage(passes, func):
-            window = ring.tile([P, S], F32, name="window", tag="window", bufs=6)
+            window = ring.tile([P, S], F32, name="window", tag="window", bufs=WINDOW_SLOTS)
             for h in range(2):
                 acc = psum.tile([P, BANK], F32, name="acc", tag="acc")
-                for a, (w_codes, w_scales, v_halves, v_scales) in enumerate(passes):
+                for kp, (lhs_codes, lhs_scales, rhs_halves, rhs_scales) in enumerate(passes):
                     nc.tensor.matmul_mx(
-                        out=acc[:], lhsT=w_codes, lhsT_scale=w_scales, rhs=v_halves[h][:].bitcast(FP8X4),
-                        rhs_scale=v_scales[:, BANK * h : BANK * (h + 1)], start=(a == 0), stop=(a == len(passes) - 1),
+                        out=acc[:], lhsT=lhs_codes, lhsT_scale=lhs_scales, rhs=rhs_halves[h][:].bitcast(FP8X4),
+                        rhs_scale=rhs_scales[:, BANK * h : BANK * (h + 1)], start=(kp == 0), stop=(kp == len(passes) - 1),
                     )
                 nc.scalar.activation(window[:, BANK * h : BANK * (h + 1)], acc[:], func)
             return window
 
-        tab2_plane = zeroed_plane(T, "tab2_plane")
-        w2_plane = zeroed_plane(S, "w2_plane")
-        tab_plane = zeroed_plane(T, "tab_plane")
-        tab3_plane = zeroed_plane(T, "tab3_plane")
-        w4_plane = zeroed_plane(GROUP, "w4_plane")
+        def side_by_side(rows):
+            return rows.rearrange("p t (pair e) -> p pair t e", e=2)
+
+        tab2_scale_tile = zeroed_scale_tile(T, "tab2_scale_tile")
+        w2_scale_tile = zeroed_scale_tile(S, "w2_scale_tile")
+        tab_scale_tile = zeroed_scale_tile(T, "tab_scale_tile")
+        tab3_scale_tile = zeroed_scale_tile(T, "tab3_scale_tile")
+        w4_scale_tile = zeroed_scale_tile(GROUP, "w4_scale_tile")
 
         offs2_sb = load_list(offs2, "offs2_sb")
         pos2_sb = load_list(pos2, "pos2_sb")
@@ -112,120 +134,134 @@ def tile_list_catalyst_cycle_oven_kernel(
         pos3_sb = load_list(pos3, "pos3_sb")
         w2_raw = held.tile([P, 2 * S], U8, name="w2_raw")
         nc.sync.dma_start(w2_raw[:].bitcast(I32), w2_words[0].bitcast(I32))
-        tab2_sb = ring.tile([P, T], U32, name="tab2_sb", tag="table", bufs=2)
-        tab2_src = tab2_words[0].rearrange("p n t -> p (n t)").bitcast(I32)
-        nc.sync.dma_start(tab2_sb[:, : T // 2].bitcast(I32), tab2_src[:, : T // 2])
-        load_scale_rows(nc.sync, tab2_plane, tab2_scales, 0)
-        nc.sync.dma_start(tab2_sb[:, T // 2 :].bitcast(I32), tab2_src[:, T // 2 :])
-        load_scale_rows(nc.sync, w2_plane, w2_scales, 0)
-        tab_sb = [ring.tile([P, T], U32, name="tab_sb", tag="table", bufs=2)]
-        tab_src = tab_words[0].rearrange("p n t -> p (n t)").bitcast(I32)
-        nc.sync.dma_start(tab_sb[0][:, : T // 2].bitcast(I32), tab_src[:, : T // 2])
-        load_scale_rows(nc.sync, tab_plane, tab_scales, 4)
-        nc.sync.dma_start(tab_sb[0][:, T // 2 :].bitcast(I32), tab_src[:, T // 2 :])
-        tab_sb.append(load_table(tab_words, 1, "tab_sb"))
-        w1_raw = {(a, 0): load_weight(w1, a, 0, "w1_raw") for a in range(2)}
+        tab2_sb = table_tile("tab2_sb")
+        load_table_columns(tab2_sb, tab2_words, 0, 0, TAB2_FIRST)
+        load_scale_rows(tab2_scale_tile, tab2_scales, 0)
+        load_table_columns(tab2_sb, tab2_words, 0, TAB2_FIRST, T)
+        load_scale_rows(w2_scale_tile, w2_scales, 0)
+        tab_sb = [table_tile("tab_sb")]
+        load_table_columns(tab_sb[0], tab_words, 0, 0, T // 2)
+        load_scale_rows(tab_scale_tile, tab_scales, V_ROW)
+        load_table_columns(tab_sb[0], tab_words, 0, T // 2, T)
+        w1_raw = {(0, 0): load_weight(w1, 0, 0, "w1_raw")}
+        tab_sb.append(table_tile("tab_sb"))
+        load_table_columns(tab_sb[1], tab_words, 1, 0, T)
+        w1_raw[1, 0] = load_weight(w1, 1, 0, "w1_raw")
         gain = held.tile([P, 2, PACK], F32, name="gain")
         nc.sync.dma_start(gain[:], gn.rearrange("(g p t) -> p g t", g=2, t=PACK))
-        for a in range(2):
-            w1_raw[a, 1] = load_weight(w1, a, 1, "w1_raw")
-        tab3_sb = load_table(tab3_words, 0, "tab3_sb")
-        load_scale_rows(nc.sync, tab3_plane, tab3_scales, 12)
+        for kp in range(2):
+            w1_raw[kp, 1] = load_weight(w1, kp, 1, "w1_raw")
+        load_scale_rows(tab3_scale_tile, tab3_scales, V3_ROW)
         w3_raw = [load_weight(w3, 0, g, "w3_raw") for g in range(2)]
-        load_scale_rows(nc.sync, w4_plane, w4_scales, 0)
+        tab3_sb = table_tile("tab3_sb")
+        load_table_columns(tab3_sb, tab3_words, 0, 0, T)
+        load_scale_rows(w4_scale_tile, w4_scales, 0)
         w4_raw = held.tile([P, 2, GROUP], I32, name="w4_raw")
-        nc.sync.dma_start(w4_raw[:], w4_words.rearrange("a p n t -> p a (n t)").bitcast(I32))
+        nc.sync.dma_start(w4_raw[:], w4_words.rearrange("kp p col i -> p kp (col i)").bitcast(I32))
+
         warm = held.tile([P, 1], F32, name="warm")
         nc.vector.memset(warm[:], 1.0)
         nc.scalar.activation(warm[:], warm[:], ACT.Abs_reciprocal_sqrt, bias=1.0)
 
-        v2_scales = gather_scales(tab2_plane, offs2_sb, "v2_scales")
+        v2_scales = gather_scales(tab2_scale_tile, offs2_sb, "v2_scales")
         w2_codes = held.tile([P, 2 * S], U8, name="w2_codes", align_bytes=64)
         nc.vector.tensor_copy(
-            w2_codes[:].rearrange("p (g t m b) -> p g t m b", g=2, t=PACK, b=2),
-            w2_raw[:].rearrange("p (g m t b) -> p g t m b", g=2, t=PACK, b=2),
+            w2_codes[:].rearrange("p (g t w byte) -> p g t w byte", g=2, t=PACK, byte=2),
+            w2_raw[:].rearrange("p (g w t byte) -> p g t w byte", g=2, t=PACK, byte=2),
         )
-        w2_dealt = held.tile([P, S], U8, name="w2_dealt", align_bytes=64)
+        w2_dealt_scales = held.tile([P, S], U8, name="w2_dealt_scales", align_bytes=64)
         nc.vector.tensor_copy(
-            w2_dealt[:].rearrange("p (g t m) -> p g t m", g=2, t=PACK),
-            w2_plane[:].rearrange("p (g m t) -> p g t m", g=2, t=PACK),
+            w2_dealt_scales[:].rearrange("p (g t w) -> p g t w", g=2, t=PACK),
+            w2_scale_tile[:].rearrange("p (g w t) -> p g t w", g=2, t=PACK),
         )
         v2 = gather_words(tab2_sb, offs2_sb, "v2")
         partial = [held.tile([P, PACK, J], F32, name="partial" + str(g)) for g in range(2)]
-        for g in range(2):
-            for t in range(PACK):
-                col = GROUP * g + P * t
-                w_codes = w2_codes[:, 2 * col : 2 * (col + P)].bitcast(FP4X4)
-                window = first_stage([(w_codes, w2_dealt[:, col : col + P], v2, v2_scales)], ACT.Copy)
-                nc.vector.tensor_copy(partial[g][:, t, :], window[:].indirect(pos2_sb[:]))
+        w1_q = {}
+        for s in range(SLICES):
+            g, t = divmod(s, PACK)
+            lhs_codes = w2_codes[:, 2 * P * s : 2 * P * (s + 1)].bitcast(FP4X4)
+            window = first_stage([(lhs_codes, w2_dealt_scales[:, P * s : P * (s + 1)], v2, v2_scales)], ACT.Copy)
+            nc.vector.tensor_copy(partial[g][:, t, :], window[:].indirect(pos2_sb[:]))
+            if s == W1_FIRST_AFTER:
+                w1_q[0, 0] = quantize_weight(w1_raw[0, 0], "w1_00")
 
-        v_scales = gather_scales(tab_plane, offs_sb, "v_scales")
-        v = [gather_words(tab_sb[a], offs_sb, "v" + str(a)) for a in range(2)]
-        picked_a = {}
-        w1_all = [[quantize_weight(w1_raw[a, g], "w1_" + str(a) + str(g), nc.scalar.copy) for a in range(2)] for g in range(2)]
-        for g in range(2):
-            w1_q = w1_all[g]
-            for t in range(PACK):
-                cols = slice(P * t, P * (t + 1))
-                passes = [
-                    (w1_q[a][0][:, cols].bitcast(FP8X4), w1_q[a][1][:, cols], v[a], v_scales[4 + 4 * a :, :])
-                    for a in (1, 0)
-                ]
-                window = first_stage(passes, ACT.Abs)
-                sat = ring.tile([P, J], F32, name="sat", tag="sat", bufs=8)
-                nc.vector.tensor_copy(sat[:], window[:].indirect(pos1_sb[:]))
-                picked_a[g, t] = sat
+        v_scales = gather_scales(tab_scale_tile, offs_sb, "v_scales")
+        v = [gather_words(tab_sb[kp], offs_sb, "v" + str(kp)) for kp in range(2)]
+        for kp, g in ((1, 0), (0, 1), (1, 1)):
+            w1_q[kp, g] = quantize_weight(w1_raw[kp, g], "w1_" + str(kp) + str(g))
+        sat = []
+        w3_q = []
+        for s in range(SLICES):
+            g, t = divmod(s, PACK)
+            cols = slice(P * t, P * (t + 1))
+            passes = [
+                (w1_q[kp, g][0][:, cols].bitcast(FP8X4), w1_q[kp, g][1][:, cols], v[kp], v_scales[V_ROW + 4 * kp :, :])
+                for kp in range(2)
+            ]
+            window = first_stage(passes, ACT.Abs)
+            sat.append(ring.tile([P, J], F32, name="sat", tag="sat", bufs=SLICES))
+            nc.vector.tensor_copy(sat[s][:], window[:].indirect(pos1_sb[:]))
+            if s % W3_EVERY == W3_EVERY - 1:
+                w3_q.append(quantize_weight(w3_raw[len(w3_q)], "w3_" + str(len(w3_q))))
 
-        v3_scales = gather_scales(tab3_plane, offs3_sb, "v3_scales")
+        v3_scales = gather_scales(tab3_scale_tile, offs3_sb, "v3_scales")
         v3 = gather_words(tab3_sb, offs3_sb, "v3")
         w4_codes = held.tile([P, 2, GROUP], I32, name="w4_codes", align_bytes=64)
         nc.vector.tensor_copy(
-            w4_codes[:].rearrange("p a (u e m) -> p a u m e", u=2, e=2),
-            w4_raw[:].rearrange("p a (m u e) -> p a u m e", u=2, e=2),
+            w4_codes[:].rearrange("p g (u e w) -> p g u w e", u=2, e=2),
+            w4_raw[:].rearrange("p g (w u e) -> p g u w e", u=2, e=2),
         )
-        w4_dealt = held.tile([P, GROUP], U8, name="w4_dealt", align_bytes=64)
+        w4_dealt_scales = held.tile([P, GROUP], U8, name="w4_dealt_scales", align_bytes=64)
         nc.vector.tensor_copy(
-            w4_dealt[:].rearrange("p (t m) -> p t m", t=PACK), w4_plane[:].rearrange("p (m t) -> p t m", t=PACK)
+            w4_dealt_scales[:].rearrange("p (t w) -> p t w", t=PACK),
+            w4_scale_tile[:].rearrange("p (w t) -> p t w", t=PACK),
         )
-        w3_q = [quantize_weight(w3_raw[g], "w3_" + str(g), (nc.vector.tensor_copy, nc.scalar.copy)[g]) for g in range(2)]
-        z_q = {}
+
+        def saturate(s):
+            g, t = divmod(s, PACK)
+            nc.scalar.activation(sat[s][:], sat[s][:], ACT.Abs_reciprocal_sqrt, bias=1.0)
+            nc.scalar.activation(sat[s][:], sat[s][:], ACT.Square)
+            nc.vector.scalar_tensor_tensor(
+                partial[g][:, t, :], sat[s][:], gain[:, g, t : t + 1], partial[g][:, t, :], ALU.mult, ALU.add
+            )
+
+        def join(g, windows, first, width, tag, slots):
+            minus_z = ring.tile([P, PACK, width], F32, name="minus_z", tag=tag, bufs=slots)
+            offsets = pos3_sb[:, first // ENTRIES : (first + width) // ENTRIES]
+            for t in range(PACK):
+                nc.vector.tensor_tensor(
+                    minus_z[:, t, :], windows[t][:].indirect(offsets), partial[g][:, t, first : first + width], ALU.subtract
+                )
+            z = ring.tile([P, PACK * width], BF16, name="z", tag="z", align_bytes=64)
+            nc.vector.tensor_scalar(
+                z[:].rearrange("p (pair e t) -> p pair t e", e=2, t=PACK), side_by_side(minus_z[:]), -1.0, None, ALU.mult
+            )
+            codes = held.tile([P, width], U32, name="z_codes" + str(g) + str(first), align_bytes=64)
+            scales = held.tile([P, width], U8, name="z_scales" + str(g) + str(first), align_bytes=64)
+            nc.vector.quantize_mx(out=codes[:].bitcast(FP8X4), scales=scales[:], in_=z[:])
+            return [(codes[:, j : j + P], scales[:, j : j + P]) for j in range(0, width, P)]
+
+        for s in range(SAT_AHEAD):
+            saturate(s)
+        z_q = []
         for g in range(2):
             windows = []
             for t in range(PACK):
                 cols = slice(P * t, P * (t + 1))
-                sat = picked_a[g, t]
-                nc.scalar.activation(sat[:], sat[:], ACT.Abs_reciprocal_sqrt, bias=1.0)
-                nc.scalar.activation(sat[:], sat[:], ACT.Square)
-                nc.vector.scalar_tensor_tensor(
-                    partial[g][:, t, :], sat[:], gain[:, g, t : t + 1], partial[g][:, t, :], ALU.mult, ALU.add
-                )
-                passes = [(w3_q[g][0][:, cols].bitcast(FP8X4), w3_q[g][1][:, cols], v3, v3_scales[12:, :])]
+                if PACK * g + t + SAT_AHEAD < SLICES:
+                    saturate(PACK * g + t + SAT_AHEAD)
+                passes = [(w3_q[g][0][:, cols].bitcast(FP8X4), w3_q[g][1][:, cols], v3, v3_scales[V3_ROW:, :])]
                 windows.append(first_stage(passes, ACT.Copy))
-            pick_width, join_width = ((512, 256), (128, 128))[g]
-            for c0 in range(0, J, pick_width):
-                picked_d = ring.tile([P, PACK, pick_width], F32, name="picked_d", tag="picked_d" + str(g), bufs=(1, 2)[g])
-                for t in range(PACK):
-                    nc.vector.tensor_tensor(
-                        picked_d[:, t, :], windows[t][:].indirect(pos3_sb[:, c0 // 16 : (c0 + pick_width) // 16]),
-                        partial[g][:, t, c0 : c0 + pick_width], ALU.subtract,
-                    )
-                for c1 in range(0, pick_width, join_width):
-                    z = ring.tile([P, PACK * join_width], BF16, name="z", tag="z", bufs=2, align_bytes=64)
-                    z_out = z[:].rearrange("p (c i t) -> p c t i", i=2, t=PACK)
-                    z_in = picked_d[:, :, c1 : c1 + join_width].rearrange("p t (c i) -> p c t i", i=2)
-                    if g in ():
-                        nc.scalar.activation(z_out, z_in, ACT.Copy, scale=-1.0)
-                    else:
-                        nc.vector.tensor_scalar(z_out, z_in, -1.0, None, ALU.mult)
-                    z_codes = held.tile([P, join_width], U32, name="z_codes" + str(g) + str(c0 + c1), align_bytes=64)
-                    z_scales = held.tile([P, join_width], U8, name="z_scales" + str(g) + str(c0 + c1), align_bytes=64)
-                    nc.vector.quantize_mx(out=z_codes[:].bitcast(FP8X4), scales=z_scales[:], in_=z[:])
-                    for c2 in range(0, join_width, P):
-                        z_q[g, (c0 + c1 + c2) // P] = (z_codes[:, c2 : c2 + P], z_scales[:, c2 : c2 + P])
+            if g == 0:
+                z_q.append(join(g, windows, 0, J, "raw", RAW_SLOTS))
+            else:
+                z_q.append([join(g, windows, first, P, "minus_z", 2)[0] for first in range(0, J, P)])
 
-        out_rows = out_0.rearrange("(p t) m -> p t m", t=PACK)
-        out_words = out_1[0].rearrange("p m t -> p (m t)").bitcast(I32)
+        out_rows = out_0.rearrange("(p t) j -> p t j", t=PACK)
+        out_words = out_1[0].rearrange("p j t -> p (j t)").bitcast(I32)
         y_scales = held.tile([P, J], U8, name="y_scales", align_bytes=64)
+        y_chunks = ring.tile([P, J // P, PACK, P], F32, name="y_chunks", tag="table", bufs=TABLE_SLOTS, align_bytes=64)
+        y_bf_chunks = ring.tile([P, J // P, P, PACK], BF16, name="y_bf_chunks", tag="table", bufs=TABLE_SLOTS, align_bytes=64)
         for c in range(J // P):
             cols = slice(P * c, P * (c + 1))
             acc = psum.tile([P, PACK, P], F32, name="y_acc", tag="acc")
@@ -233,25 +269,25 @@ def tile_list_catalyst_cycle_oven_kernel(
                 for g in (1, 0):
                     nc.tensor.matmul_mx(
                         out=acc[:, t, :], lhsT=w4_codes[:, g, P * t : P * (t + 1)].bitcast(FP8X4),
-                        lhsT_scale=w4_dealt[4 * g :, P * t : P * (t + 1)], rhs=z_q[g, c][0].bitcast(FP8X4),
-                        rhs_scale=z_q[g, c][1], start=(g == 1), stop=(g == 0),
+                        lhsT_scale=w4_dealt_scales[4 * g :, P * t : P * (t + 1)], rhs=z_q[g][c][0].bitcast(FP8X4),
+                        rhs_scale=z_q[g][c][1], start=(g == 1), stop=(g == 0),
                     )
-            y_bf = ring.tile([P, P, PACK], BF16, name="y_bf", tag="y_bf", bufs=4, align_bytes=64)
-            y = ring.tile([P, PACK, P], F32, name="y", tag="y", bufs=4)
-            if c >= 0:
+            y = y_chunks[:, c]
+            y_bf = y_bf_chunks[:, c]
+            if c < Y_BY_SCALAR:
+                nc.scalar.copy(y_bf[:], acc[:].rearrange("p t j -> p j t"))
                 nc.scalar.copy(y[:], acc[:])
-                nc.vector.tensor_copy(
-                    y_bf[:].rearrange("p (c i) t -> p c t i", i=2), y[:].rearrange("p t (c i) -> p c t i", i=2)
-                )
             else:
-                nc.scalar.copy(y_bf[:], acc[:].rearrange("p t m -> p m t"))
                 nc.scalar.copy(y[:], acc[:])
+                nc.vector.tensor_copy(y_bf[:].rearrange("p (pair e) t -> p pair t e", e=2), side_by_side(y[:]))
             nc.sync.dma_start(out_rows[:, :, cols], y[:])
             y_codes = held.tile([P, P], U32, name="y_codes" + str(c), align_bytes=64)
             nc.vector.quantize_mx(
-                out=y_codes[:].bitcast(FP8X4), scales=y_scales[:, cols], in_=y_bf[:].rearrange("p m t -> p (m t)")
+                out=y_codes[:].bitcast(FP8X4), scales=y_scales[:, cols], in_=y_bf[:].rearrange("p j t -> p (j t)")
             )
             nc.sync.dma_start(out_words[:, cols], y_codes[:].bitcast(I32))
-        for q in range(4):
-            queue = nc.sync if q % 2 == 0 else nc.scalar
-            queue.dma_start(out_2[0, 4 * q : 4 * q + 4, :].bitcast(I32), y_scales[32 * q : 32 * q + 4, :].bitcast(I32))
+        for quad in range(4):
+            queue = nc.sync if quad % 2 == 0 else nc.scalar
+            queue.dma_start(
+                out_2[0, 4 * quad : 4 * quad + 4, :].bitcast(I32), y_scales[32 * quad : 32 * quad + 4, :].bitcast(I32)
+            )

from contextlib import ExitStack

import concourse.mybir as mybir

F32 = mybir.dt.float32
BF16 = mybir.dt.bfloat16
I32 = mybir.dt.int32
U32 = mybir.dt.uint32
U16 = mybir.dt.uint16
U8 = mybir.dt.uint8
FP8X4 = mybir.dt.float8_e4m3fn_x4
FP4X4 = mybir.dt.float4_e2m1fn_x4
ACT = mybir.ActivationFunctionType
ALU = mybir.AluOpType

FLOPS = 4831838208

P = 128
PACK = 4
GROUP = P * PACK
T = 4096
S = 1024
J = 512
BANK = 512
ENTRIES = 16
SLICES = 2 * PACK

V_ROW, V3_ROW = 4, 12

TABLE_SLOTS = 3
RAW_SLOTS = 4
ROUNDED_SLOTS = 4
WINDOW_SLOTS = 7

TAB2_FIRST = T // 4
W1_FIRST_AFTER = 5
W3_EVERY = 3
SAT_AHEAD = 2
Y_BY_SCALAR = 2


def tile_list_catalyst_cycle_oven_kernel(
    tc, tab_words, tab_scales, tab2_words, tab2_scales, tab3_words, tab3_scales, offs, offs2, offs3,
    pos1, pos2, pos3, w1, w2_words, w2_scales, w3, gn, w4_words, w4_scales, out_0, out_1, out_2,
):
    nc = tc.nc
    with ExitStack() as ctx:
        held = ctx.enter_context(tc.tile_pool(name="held", bufs=1))
        ring = ctx.enter_context(tc.tile_pool(name="ring", bufs=2))
        psum = ctx.enter_context(tc.psum_pool(name="psum", bufs=8))

        def load_list(src, name):
            lst = held.tile(list(src.shape), U16, name=name)
            nc.sync.dma_start(lst[:], src)
            return lst

        def zeroed_scale_tile(width, name):
            tile = held.tile([P, width], U8, name=name, align_bytes=64)
            nc.vector.memset(tile[:].bitcast(I32), 0)
            return tile

        def load_scale_rows(tile, src, first_row):
            passes = src.shape[0]
            for quad in range(4):
                row = 32 * quad + first_row
                nc.sync.dma_start(
                    tile[row : row + 4 * passes, :].bitcast(I32), src[:, 4 * quad : 4 * quad + 4, :].bitcast(I32)
                )

        def table_tile(name):
            return ring.tile([P, T], U32, name=name, tag="table", bufs=TABLE_SLOTS, align_bytes=64)

        def load_table_columns(words, src, kp, first, last):
            columns = src[kp].rearrange("p col i -> p (col i)").bitcast(I32)
            nc.sync.dma_start(words[:, first:last].bitcast(I32), columns[:, first:last])

        def load_weight(src, kp, g, name):
            raw = ring.tile([P, PACK, GROUP], F32, name=name, tag="raw", bufs=RAW_SLOTS)
            rows = src[GROUP * kp : GROUP * (kp + 1), GROUP * g : GROUP * (g + 1)]
            nc.sync.dma_start(raw[:], rows.rearrange("(p i) col -> p i col", i=PACK))
            return raw

        def gather_scales(tile, lst, name):
            picked = held.tile([P, S], U8, name=name, align_bytes=64)
            nc.vector.tensor_copy(picked[:], tile[:].indirect(lst[:]))
            return picked

        def gather_words(words, lst, name):
            halves = []
            width = BANK // ENTRIES
            for h in range(2):
                picked = held.tile([P, BANK], U32, name=name + str(h), align_bytes=64)
                nc.vector.tensor_copy(picked[:], words[:].indirect(lst[:, width * h : width * (h + 1)]))
                halves.append(picked)
            return halves

        def quantize_weight(raw, name):
            rounded = ring.tile([P, PACK * GROUP], BF16, name="rounded", tag="rounded", bufs=ROUNDED_SLOTS, align_bytes=64)
            nc.scalar.copy(
                rounded[:].rearrange("p (u e w i) -> p u w i e", u=2, e=2, i=PACK),
                raw[:].rearrange("p i (w u e) -> p u w i e", u=2, e=2),
            )
            codes = held.tile([P, GROUP], U32, name=name + "_codes", align_bytes=64)
            scales = held.tile([P, GROUP], U8, name=name + "_scales", align_bytes=64)
            nc.vector.quantize_mx(out=codes[:].bitcast(FP8X4), scales=scales[:], in_=rounded[:])
            return codes, scales

        def first_stage(passes, func):
            window = ring.tile([P, S], F32, name="window", tag="window", bufs=WINDOW_SLOTS)
            for h in range(2):
                acc = psum.tile([P, BANK], F32, name="acc", tag="acc")
                for kp, (lhs_codes, lhs_scales, rhs_halves, rhs_scales) in enumerate(passes):
                    nc.tensor.matmul_mx(
                        out=acc[:], lhsT=lhs_codes, lhsT_scale=lhs_scales, rhs=rhs_halves[h][:].bitcast(FP8X4),
                        rhs_scale=rhs_scales[:, BANK * h : BANK * (h + 1)], start=(kp == 0), stop=(kp == len(passes) - 1),
                    )
                nc.scalar.activation(window[:, BANK * h : BANK * (h + 1)], acc[:], func)
            return window

        def side_by_side(rows):
            return rows.rearrange("p t (pair e) -> p pair t e", e=2)

        tab2_scale_tile = zeroed_scale_tile(T, "tab2_scale_tile")
        w2_scale_tile = zeroed_scale_tile(S, "w2_scale_tile")
        tab_scale_tile = zeroed_scale_tile(T, "tab_scale_tile")
        tab3_scale_tile = zeroed_scale_tile(T, "tab3_scale_tile")
        w4_scale_tile = zeroed_scale_tile(GROUP, "w4_scale_tile")

        offs2_sb = load_list(offs2, "offs2_sb")
        pos2_sb = load_list(pos2, "pos2_sb")
        offs_sb = load_list(offs, "offs_sb")
        pos1_sb = load_list(pos1, "pos1_sb")
        offs3_sb = load_list(offs3, "offs3_sb")
        pos3_sb = load_list(pos3, "pos3_sb")
        w2_raw = held.tile([P, 2 * S], U8, name="w2_raw")
        nc.sync.dma_start(w2_raw[:].bitcast(I32), w2_words[0].bitcast(I32))
        tab2_sb = table_tile("tab2_sb")
        load_table_columns(tab2_sb, tab2_words, 0, 0, TAB2_FIRST)
        load_scale_rows(tab2_scale_tile, tab2_scales, 0)
        load_table_columns(tab2_sb, tab2_words, 0, TAB2_FIRST, T)
        load_scale_rows(w2_scale_tile, w2_scales, 0)
        tab_sb = [table_tile("tab_sb")]
        load_table_columns(tab_sb[0], tab_words, 0, 0, T // 2)
        load_scale_rows(tab_scale_tile, tab_scales, V_ROW)
        load_table_columns(tab_sb[0], tab_words, 0, T // 2, T)
        w1_raw = {(0, 0): load_weight(w1, 0, 0, "w1_raw")}
        tab_sb.append(table_tile("tab_sb"))
        load_table_columns(tab_sb[1], tab_words, 1, 0, T)
        w1_raw[1, 0] = load_weight(w1, 1, 0, "w1_raw")
        gain = held.tile([P, 2, PACK], F32, name="gain")
        nc.sync.dma_start(gain[:], gn.rearrange("(g p t) -> p g t", g=2, t=PACK))
        for kp in range(2):
            w1_raw[kp, 1] = load_weight(w1, kp, 1, "w1_raw")
        load_scale_rows(tab3_scale_tile, tab3_scales, V3_ROW)
        w3_raw = [load_weight(w3, 0, g, "w3_raw") for g in range(2)]
        tab3_sb = table_tile("tab3_sb")
        load_table_columns(tab3_sb, tab3_words, 0, 0, T)
        load_scale_rows(w4_scale_tile, w4_scales, 0)
        w4_raw = held.tile([P, 2, GROUP], I32, name="w4_raw")
        nc.sync.dma_start(w4_raw[:], w4_words.rearrange("kp p col i -> p kp (col i)").bitcast(I32))

        warm = held.tile([P, 1], F32, name="warm")
        nc.vector.memset(warm[:], 1.0)
        nc.scalar.activation(warm[:], warm[:], ACT.Abs_reciprocal_sqrt, bias=1.0)

        v2_scales = gather_scales(tab2_scale_tile, offs2_sb, "v2_scales")
        w2_codes = held.tile([P, 2 * S], U8, name="w2_codes", align_bytes=64)
        nc.vector.tensor_copy(
            w2_codes[:].rearrange("p (g t w byte) -> p g t w byte", g=2, t=PACK, byte=2),
            w2_raw[:].rearrange("p (g w t byte) -> p g t w byte", g=2, t=PACK, byte=2),
        )
        w2_dealt_scales = held.tile([P, S], U8, name="w2_dealt_scales", align_bytes=64)
        nc.vector.tensor_copy(
            w2_dealt_scales[:].rearrange("p (g t w) -> p g t w", g=2, t=PACK),
            w2_scale_tile[:].rearrange("p (g w t) -> p g t w", g=2, t=PACK),
        )
        v2 = gather_words(tab2_sb, offs2_sb, "v2")
        partial = [held.tile([P, PACK, J], F32, name="partial" + str(g)) for g in range(2)]
        w1_q = {}
        for s in range(SLICES):
            g, t = divmod(s, PACK)
            lhs_codes = w2_codes[:, 2 * P * s : 2 * P * (s + 1)].bitcast(FP4X4)
            window = first_stage([(lhs_codes, w2_dealt_scales[:, P * s : P * (s + 1)], v2, v2_scales)], ACT.Copy)
            nc.vector.tensor_copy(partial[g][:, t, :], window[:].indirect(pos2_sb[:]))
            if s == W1_FIRST_AFTER:
                w1_q[0, 0] = quantize_weight(w1_raw[0, 0], "w1_00")

        v_scales = gather_scales(tab_scale_tile, offs_sb, "v_scales")
        v = [gather_words(tab_sb[kp], offs_sb, "v" + str(kp)) for kp in range(2)]
        for kp, g in ((1, 0), (0, 1), (1, 1)):
            w1_q[kp, g] = quantize_weight(w1_raw[kp, g], "w1_" + str(kp) + str(g))
        sat = []
        w3_q = []
        for s in range(SLICES):
            g, t = divmod(s, PACK)
            cols = slice(P * t, P * (t + 1))
            passes = [
                (w1_q[kp, g][0][:, cols].bitcast(FP8X4), w1_q[kp, g][1][:, cols], v[kp], v_scales[V_ROW + 4 * kp :, :])
                for kp in range(2)
            ]
            window = first_stage(passes, ACT.Abs)
            sat.append(ring.tile([P, J], F32, name="sat", tag="sat", bufs=SLICES))
            nc.vector.tensor_copy(sat[s][:], window[:].indirect(pos1_sb[:]))
            if s % W3_EVERY == W3_EVERY - 1:
                w3_q.append(quantize_weight(w3_raw[len(w3_q)], "w3_" + str(len(w3_q))))

        v3_scales = gather_scales(tab3_scale_tile, offs3_sb, "v3_scales")
        v3 = gather_words(tab3_sb, offs3_sb, "v3")
        w4_codes = held.tile([P, 2, GROUP], I32, name="w4_codes", align_bytes=64)
        nc.vector.tensor_copy(
            w4_codes[:].rearrange("p g (u e w) -> p g u w e", u=2, e=2),
            w4_raw[:].rearrange("p g (w u e) -> p g u w e", u=2, e=2),
        )
        w4_dealt_scales = held.tile([P, GROUP], U8, name="w4_dealt_scales", align_bytes=64)
        nc.vector.tensor_copy(
            w4_dealt_scales[:].rearrange("p (t w) -> p t w", t=PACK),
            w4_scale_tile[:].rearrange("p (w t) -> p t w", t=PACK),
        )

        def saturate(s):
            g, t = divmod(s, PACK)
            nc.scalar.activation(sat[s][:], sat[s][:], ACT.Abs_reciprocal_sqrt, bias=1.0)
            nc.scalar.activation(sat[s][:], sat[s][:], ACT.Square)
            nc.vector.scalar_tensor_tensor(
                partial[g][:, t, :], sat[s][:], gain[:, g, t : t + 1], partial[g][:, t, :], ALU.mult, ALU.add
            )

        def join(g, windows, first, width, tag, slots):
            minus_z = ring.tile([P, PACK, width], F32, name="minus_z", tag=tag, bufs=slots)
            offsets = pos3_sb[:, first // ENTRIES : (first + width) // ENTRIES]
            for t in range(PACK):
                nc.vector.tensor_tensor(
                    minus_z[:, t, :], windows[t][:].indirect(offsets), partial[g][:, t, first : first + width], ALU.subtract
                )
            z = ring.tile([P, PACK * width], BF16, name="z", tag="z", align_bytes=64)
            nc.vector.tensor_scalar(
                z[:].rearrange("p (pair e t) -> p pair t e", e=2, t=PACK), side_by_side(minus_z[:]), -1.0, None, ALU.mult
            )
            codes = held.tile([P, width], U32, name="z_codes" + str(g) + str(first), align_bytes=64)
            scales = held.tile([P, width], U8, name="z_scales" + str(g) + str(first), align_bytes=64)
            nc.vector.quantize_mx(out=codes[:].bitcast(FP8X4), scales=scales[:], in_=z[:])
            return [(codes[:, j : j + P], scales[:, j : j + P]) for j in range(0, width, P)]

        for s in range(SAT_AHEAD):
            saturate(s)
        z_q = []
        for g in range(2):
            windows = []
            for t in range(PACK):
                cols = slice(P * t, P * (t + 1))
                if PACK * g + t + SAT_AHEAD < SLICES:
                    saturate(PACK * g + t + SAT_AHEAD)
                passes = [(w3_q[g][0][:, cols].bitcast(FP8X4), w3_q[g][1][:, cols], v3, v3_scales[V3_ROW:, :])]
                windows.append(first_stage(passes, ACT.Copy))
            if g == 0:
                z_q.append(join(g, windows, 0, J, "raw", RAW_SLOTS))
            else:
                z_q.append([join(g, windows, first, P, "minus_z", 2)[0] for first in range(0, J, P)])

        out_rows = out_0.rearrange("(p t) j -> p t j", t=PACK)
        out_words = out_1[0].rearrange("p j t -> p (j t)").bitcast(I32)
        y_scales = held.tile([P, J], U8, name="y_scales", align_bytes=64)
        y_chunks = ring.tile([P, J // P, PACK, P], F32, name="y_chunks", tag="table", bufs=TABLE_SLOTS, align_bytes=64)
        y_bf_chunks = ring.tile([P, J // P, P, PACK], BF16, name="y_bf_chunks", tag="table", bufs=TABLE_SLOTS, align_bytes=64)
        for c in range(J // P):
            cols = slice(P * c, P * (c + 1))
            acc = psum.tile([P, PACK, P], F32, name="y_acc", tag="acc")
            for t in range(PACK):
                for g in (1, 0):
                    nc.tensor.matmul_mx(
                        out=acc[:, t, :], lhsT=w4_codes[:, g, P * t : P * (t + 1)].bitcast(FP8X4),
                        lhsT_scale=w4_dealt_scales[4 * g :, P * t : P * (t + 1)], rhs=z_q[g][c][0].bitcast(FP8X4),
                        rhs_scale=z_q[g][c][1], start=(g == 1), stop=(g == 0),
                    )
            y = y_chunks[:, c]
            y_bf = y_bf_chunks[:, c]
            if c < Y_BY_SCALAR:
                nc.scalar.copy(y_bf[:], acc[:].rearrange("p t j -> p j t"))
                nc.scalar.copy(y[:], acc[:])
            else:
                nc.scalar.copy(y[:], acc[:])
                nc.vector.tensor_copy(y_bf[:].rearrange("p (pair e) t -> p pair t e", e=2), side_by_side(y[:]))
            nc.sync.dma_start(out_rows[:, :, cols], y[:])
            y_codes = held.tile([P, P], U32, name="y_codes" + str(c), align_bytes=64)
            nc.vector.quantize_mx(
                out=y_codes[:].bitcast(FP8X4), scales=y_scales[:, cols], in_=y_bf[:].rearrange("p j t -> p (j t)")
            )
            nc.sync.dma_start(out_words[:, cols], y_codes[:].bitcast(I32))
        for quad in range(4):
            queue = nc.sync if quad % 2 == 0 else nc.scalar
            queue.dma_start(
                out_2[0, 4 * quad : 4 * quad + 4, :].bitcast(I32), y_scales[32 * quad : 32 * quad + 4, :].bitcast(I32)
            )
